import numpy as np
import ml_dtypes


def mxq(x, axis, fmt="e4m3"):
    dtype, down = {"e4m3": (ml_dtypes.float8_e4m3fn, 7), "e5m2": (ml_dtypes.float8_e5m2, 14)}[fmt]
    v = np.moveaxis(np.asarray(x, np.float32).astype(ml_dtypes.bfloat16).astype(np.float64), axis, -1)
    blocks = v.reshape(v.shape[:-1] + (-1, 32))
    amax = np.abs(blocks).max(-1, keepdims=True)
    byte = np.maximum(np.where(amax > 0, np.frexp(amax)[1] - 1 + 127, 0) - down, 1)
    scale = np.exp2(byte - 127.0)
    codes = (blocks / scale).astype(np.float32).astype(dtype).astype(np.float64)
    return np.moveaxis((codes * scale).reshape(v.shape), -1, axis)


WIDE = False


def mx_kscale(k):
    if not WIDE:
        return np.ones(k)
    levels = np.array([10, -10, 5, -5, 0])
    if k % 512:
        return np.exp2(np.random.permutation(np.resize(levels, k // 32))).repeat(32)
    a = np.empty((k // 512, 16))
    for p in range(k // 512):
        a[p, :8] = np.random.permutation(np.resize(levels, 8))
        for g in range(8):
            far = levels[np.abs(levels - a[p, g]) >= 10]
            a[p, g + 8] = far[np.random.randint(len(far))]
    return np.exp2(a.ravel()).repeat(32)


def f64(x):
    return np.asarray(x).astype(np.float64)


def striped8(idx):
    return np.concatenate([x.reshape(-1, 16).T for x in idx]).astype(np.uint16)


def runs(offs, k):
    lists = np.stack([offs[16 * r : 16 * r + 16].T.reshape(-1) for r in range(8)]).astype(np.int64)
    return lists[np.arange(k) % 512 // 64]


def pack_weight(w):
    k, n = w.shape
    w = f64(np.asarray(w, np.float32).astype(ml_dtypes.bfloat16)).reshape(k // 32, 32, n)
    amax = np.abs(w).max(1)
    byte = np.clip(np.where(amax > 0, np.frexp(amax)[1] - 1 + 127 - 7, 1), 1, 254)
    scaled = (w * np.exp2(127.0 - byte)[:, None, :]).reshape(k, n).astype(np.float32)
    words = np.ascontiguousarray(scaled.reshape(k // 512, 128, 4, n).transpose(0, 1, 3, 2)).astype(ml_dtypes.float8_e4m3fn).view(np.uint8)
    return words, np.ascontiguousarray(byte.astype(np.uint8).reshape(k // 512, 16, n))


def unpack_weight(words, scales):
    g, p, n, _ = words.shape
    vals = np.ascontiguousarray(words).view(ml_dtypes.float8_e4m3fn).astype(np.float64) * np.repeat(np.exp2(scales.astype(np.float64) - 127.0), 8, axis=1)[..., None]
    return vals.transpose(0, 1, 3, 2).reshape(g * 512, n)


E2M1 = np.array([0.0, 0.5, 1.0, 1.5, 2.0, 3.0, 4.0, 6.0, -0.0, -0.5, -1.0, -1.5, -2.0, -3.0, -4.0, -6.0])


def pack_fp4(w):
    k, n = w.shape
    w = f64(np.asarray(w, np.float32).astype(ml_dtypes.bfloat16)).reshape(k // 32, 32, n)
    amax = np.abs(w).max(1)
    mant, ex = np.frexp(amax / 6.0)
    byte = np.clip(np.where(amax > 0, np.where(mant > 0.5, ex, ex - 1) + 127, 1), 1, 254)
    scaled = (w * np.exp2(127.0 - byte)[:, None, :]).reshape(k, n).astype(np.float32)
    c = np.ascontiguousarray(scaled.reshape(k // 512, 128, 4, n).transpose(0, 1, 3, 2)).astype(ml_dtypes.float4_e2m1fn).view(np.uint8) & 0xF
    words = (c[..., 0::2] | (c[..., 1::2] << 4)).reshape(k // 512, 128, 2 * n)
    return np.ascontiguousarray(words), np.ascontiguousarray(byte.astype(np.uint8).reshape(k // 512, 16, n))


def unpack_fp4(words, scales):
    g, _, n = scales.shape
    words = np.ascontiguousarray(words).reshape(g, 128, n, 2)
    nib = np.empty((g, 128, n, 4), np.uint8)
    nib[..., 0::2] = words & 0xF
    nib[..., 1::2] = words >> 4
    vals = E2M1[nib] * np.repeat(np.exp2(scales.astype(np.float64) - 127.0), 8, axis=1)[..., None]
    return vals.transpose(0, 1, 3, 2).reshape(g * 512, n)


K, T, S, N, G, H, W = 512, 2048, 512, 512, 2048, 512, 256


def setup_inputs():
    n = np.random.standard_normal
    s = mx_kscale(K)[:, None]
    u = mx_kscale(S)
    packed_xT = pack_weight(n((K, T)) * s)
    packed_dT = pack_weight(n((K, G)) / s)
    packed_w1 = pack_fp4(n((H, N)) / np.sqrt(H) / u[:, None])
    perm = np.stack([np.random.permutation(S) for _ in range(8)])
    return {
        "x_words": packed_xT[0],
        "x_scales": packed_xT[1],
        "d_words": packed_dT[0],
        "d_scales": packed_dT[1],
        "gn": (np.random.uniform(0.5, 1.5, (H, 1)) * u[:, None]).astype(np.float32),
        "w1_words": packed_w1[0],
        "w1_scales": packed_w1[1],
        "offs": striped8(np.random.randint(0, T, (8, S))),
        "k1": striped8(np.random.randint(0, G, (8, H))),
        "n1": striped8(perm[:, :W]),
        "n2": striped8(perm[:, W:]),
        "n3": striped8(np.stack([np.random.permutation(S) for _ in range(8)])),
    }


def reference(x_words, x_scales, d_words, d_scales, gn, w1_words, w1_scales, offs, k1, n1, n2, n3):
    d_k1 = unpack_weight(d_words, d_scales)[np.arange(K)[:, None], runs(k1, K)]
    xq = unpack_weight(x_words, x_scales)[np.arange(K)[:, None], runs(offs, K)]
    h = 0.0625 * (d_k1.T @ xq)
    z = f64(gn) * h
    h2 = unpack_fp4(w1_words, w1_scales).T @ mxq(z, 0, "e4m3")
    pa = h2[np.arange(N)[:, None], runs(n1, N)]
    pb = h2[np.arange(N)[:, None], runs(n2, N)]
    rb = pa - pb
    ra = pa + pb
    ds = np.zeros((N, S))
    ds[np.arange(N)[:, None], runs(n1, N)] = ra
    dt = ds.copy()
    dt[np.arange(N)[:, None], runs(n2, N)] = rb
    return np.maximum(dt, dt[np.arange(N)[:, None], runs(n3, N)])

@@ -1,0 +1,228 @@
+from contextlib import ExitStack
+
+import concourse.mybir as mybir
+
+F32 = mybir.dt.float32
+BF16 = mybir.dt.bfloat16
+I32 = mybir.dt.int32
+U32 = mybir.dt.uint32
+U16 = mybir.dt.uint16
+U8 = mybir.dt.uint8
+FP8X4 = mybir.dt.float8_e4m3fn_x4
+FP4X4 = mybir.dt.float4_e2m1fn_x4
+COPY = mybir.ActivationFunctionType.Copy
+ADD = mybir.AluOpType.add
+MULT = mybir.AluOpType.mult
+MAX = mybir.AluOpType.max
+
+P = 128
+PACK = 4
+TABLE = 2048
+S = 512
+PAIRS = 256
+BLOCK = 128
+LIST_ROWS = 16
+
+FLOPS = 2 * 2 * 512 * 512 * 512
+
+
+def tile_picked_hpqihaarh_none_p_kernel(
+    tc, x_words, x_scales, d_words, d_scales, gn, w1_words, w1_scales, offs, k1, n1, n2, n3, out
+):
+    nc = tc.nc
+    with ExitStack() as ctx:
+        keep = ctx.enter_context(tc.tile_pool(name="keep", bufs=1))
+        psum = ctx.enter_context(tc.psum_pool(name="psum", bufs=1))
+
+        def sbuf(name, columns, dtype):
+            return keep.tile([P, columns], dtype, name=name, align_bytes=64)
+
+        def load_list(name, dram):
+            tile = keep.tile(list(dram.shape), U16, name=name)
+            nc.sync.dma_start(tile[:], dram)
+            return tile
+
+        def entries(list_tile, first, count):
+            return list_tile[:, first // LIST_ROWS : (first + count) // LIST_ROWS]
+
+        xs_table = sbuf("xs_table", TABLE, U8)
+        ds_table = sbuf("ds_table", TABLE, U8)
+        w_scale_raw = sbuf("w_scale_raw", S, U8)
+        w_scale_spread = sbuf("w_scale_spread", S, U8)
+        w_scale = sbuf("w_scale", S, U8)
+        planes = sbuf("planes", 2 * S, U8)
+        gain_raw = sbuf("gain_raw", PACK, F32)
+        w_word_raw = sbuf("w_word_raw", 2 * S, U8)
+        dw_table = sbuf("dw_table", TABLE, I32)
+        xw_table = sbuf("xw_table", TABLE, I32)
+
+        def load_scale_rows(queue, tile, rows):
+            words = rows.shape[1] // 4
+            queue.dma_start(tile[:].bitcast(I32), rows.bitcast(I32).unsqueeze(1).to_broadcast([16, 8, words]))
+
+        def place_scale_rows(queue, plane, spread_rows):
+            for a in range(4):
+                queue.dma_start(plane[a:P:32, :].bitcast(I32), spread_rows[8 * a : P : 32, :].bitcast(I32))
+
+        nc.gpsimd.memset(planes[:].bitcast(I32), 0)
+        nc.gpsimd.memset(w_scale[:].bitcast(I32), 0)
+        nc.gpsimd.dma_start(gain_raw[:], gn.rearrange("(p t) o -> p (t o)", t=PACK))
+        load_scale_rows(nc.scalar, w_scale_raw, w1_scales[0])
+        nc.scalar.dma_start(w_word_raw[:].bitcast(I32), w1_words[0].bitcast(I32))
+        k1_t = load_list("k1_t", k1)
+        load_scale_rows(nc.sync, ds_table, d_scales[0])
+        offs_t = load_list("offs_t", offs)
+        load_scale_rows(nc.sync, xs_table, x_scales[0])
+        nc.sync.dma_start(dw_table[:], d_words[0].rearrange("p c r -> p (c r)").bitcast(I32))
+        nc.sync.dma_start(xw_table[:], x_words[0].rearrange("p c r -> p (c r)").bitcast(I32))
+        n1_t = load_list("n1_t", n1)
+        n2_t = load_list("n2_t", n2)
+        n3_t = load_list("n3_t", n3)
+        nc.vector.tensor_copy(
+            w_scale_spread[:].rearrange("p (t m) -> p t m", t=PACK),
+            w_scale_raw[:].rearrange("p (m t) -> p t m", t=PACK),
+        )
+        place_scale_rows(nc.gpsimd, w_scale, w_scale_spread)
+
+        ds_picked = sbuf("ds_picked", S, U8)
+        xs_picked = sbuf("xs_picked", S, U8)
+        spread = sbuf("spread", 2 * S, U8)
+        nc.vector.tensor_copy(ds_picked[:], ds_table[:].indirect(k1_t[:]))
+        nc.vector.tensor_copy(xs_picked[:], xs_table[:].indirect(offs_t[:]))
+        nc.vector.tensor_copy(
+            spread[:, 0:S].rearrange("p (t m) -> p t m", t=PACK),
+            ds_picked[:].rearrange("p (m t) -> p t m", t=PACK),
+        )
+        nc.vector.tensor_copy(spread[:, S : 2 * S].bitcast(I32), xs_picked[:].bitcast(I32))
+        place_scale_rows(nc.scalar, planes, spread)
+
+        dw_picked = sbuf("dw_picked", S, U32)
+        dw_dealt = sbuf("dw_dealt", S, U32)
+        nc.vector.tensor_copy(dw_picked[:], dw_table[:].bitcast(U32).indirect(k1_t[:]))
+        nc.vector.tensor_copy(
+            dw_dealt[:].rearrange("p (t c i) -> p c t i", t=PACK, i=4),
+            dw_picked[:].rearrange("p (c i t) -> p c t i", t=PACK, i=4),
+        )
+        xw_picked = [sbuf("xw_picked%d" % half, S // 2, U32) for half in range(2)]
+        for half in range(2):
+            nc.vector.tensor_copy(
+                xw_picked[half][:],
+                xw_table[:].bitcast(U32).indirect(entries(offs_t, half * (S // 2), S // 2)),
+            )
+
+        gain = sbuf("gain", PACK, F32)
+        nc.scalar.activation(gain[:], gain_raw[:], COPY, scale=0.0625)
+        w_word = sbuf("w_word", 2 * S, U8)
+        nc.scalar.copy(
+            w_word[:].bitcast(U16).rearrange("p (t m) -> p t m", t=PACK),
+            w_word_raw[:].bitcast(U16).rearrange("p (m t) -> p t m", t=PACK),
+        )
+
+        blocks = S // BLOCK
+        z = [sbuf("z%d" % b, PACK * BLOCK, BF16) for b in range(blocks)]
+        z_word = sbuf("z_word", S, U32)
+        z_scale = sbuf("z_scale", S, U8)
+        for b in range(blocks):
+            h = psum.tile([P, PACK, BLOCK], F32, name="h%d" % b, tag="bank%d" % b)
+            half, inner = divmod(b, 2)
+            for t in range(PACK):
+                nc.tensor.matmul_mx(
+                    h[:, t, :],
+                    lhsT=dw_dealt[:, t * P : (t + 1) * P].bitcast(FP8X4),
+                    lhsT_scale=planes[:, t * P : (t + 1) * P],
+                    rhs=xw_picked[half][:, inner * BLOCK : (inner + 1) * BLOCK].bitcast(FP8X4),
+                    rhs_scale=planes[:, S + b * BLOCK : S + (b + 1) * BLOCK],
+                    start=True,
+                    stop=True,
+                )
+            z_jt = z[b][:].rearrange("p (j t) -> p j t", t=PACK)
+            if b == 0:
+                for t in range(PACK):
+                    nc.scalar.activation(z_jt[:, :, t], h[:, t, :], COPY, scale=gain[:, t : t + 1])
+            else:
+                nc.vector.tensor_tensor(
+                    z_jt,
+                    h[:].rearrange("p t j -> p j t"),
+                    gain[:].unsqueeze(1).to_broadcast([P, BLOCK, PACK]),
+                    MULT,
+                )
+        for b in (1, 2, 0, 3):
+            cols = slice(b * BLOCK, (b + 1) * BLOCK)
+            nc.vector.quantize_mx(z_word[:, cols].bitcast(FP8X4), z_scale[:, cols], z[b][:])
+
+        def second(acc, t, first, count):
+            nc.tensor.matmul_mx(
+                acc,
+                lhsT=w_word[:, 2 * t * P : 2 * (t + 1) * P].bitcast(FP4X4),
+                lhsT_scale=w_scale[:, t * P : (t + 1) * P],
+                rhs=z_word[:, first : first + count].bitcast(FP8X4),
+                rhs_scale=z_scale[:, first : first + count],
+                start=True,
+                stop=True,
+            )
+
+        h2 = [sbuf("h2_%d" % t, S, F32) for t in range(PACK)]
+        pa = [sbuf("pa%d" % t, PAIRS, F32) for t in range(PACK)]
+        pb = [sbuf("pb%d" % t, PAIRS, F32) for t in range(PACK)]
+        neg_pb = [sbuf("neg_pb%d" % t, PAIRS, F32) for t in range(PACK)]
+        dt = [sbuf("dt%d" % t, S, F32) for t in range(PACK)]
+        partner = [sbuf("partner%d" % t, S, F32) for t in range(PACK)]
+        result = [sbuf("result%d" % t, S, F32) for t in range(PACK)]
+        out_t = out.rearrange("(p t) j -> t p j", t=PACK)
+
+        early = psum.tile([P, S - BLOCK], F32, name="early", tag="bank4")
+        late = psum.tile([P, BLOCK], F32, name="late", tag="bank5")
+        for b in (1, 2, 0):
+            second(early[:, b * BLOCK : (b + 1) * BLOCK], 0, b * BLOCK, BLOCK)
+        second(late[:], 0, S - BLOCK, BLOCK)
+        acc2 = [None]
+        for t in range(1, PACK):
+            acc = psum.tile([P, S], F32, name="acc%d" % t, tag=("bank6", "bank7", "bank0")[t - 1])
+            second(acc[:], t, 0, S)
+            acc2.append(acc)
+
+        def fetch_pairs(t):
+            if t == 0:
+                nc.scalar.copy(h2[0][:, 0 : S - BLOCK], early[:])
+                nc.scalar.copy(h2[0][:, S - BLOCK : S], late[:])
+                nc.vector.tensor_copy(pa[0][:], h2[0][:].indirect(n1_t[:]))
+            else:
+                nc.scalar.copy(h2[t][:], acc2[t][:])
+                nc.scalar.activation(pa[t][:], h2[t][:].indirect(n1_t[:]), COPY)
+            nc.scalar.activation(pb[t][:], h2[t][:].indirect(n2_t[:]), COPY)
+
+        def put_sums(t):
+            nc.vector.tensor_tensor(dt[t][:].indirect(n1_t[:]), pa[t][:], pb[t][:], ADD)
+
+        def put_differences(t):
+            nc.scalar.activation(neg_pb[t][:], pb[t][:], COPY, scale=-1.0)
+            nc.vector.tensor_tensor(dt[t][:].indirect(n2_t[:]), pa[t][:], neg_pb[t][:], ADD)
+
+        def finish(t, pieces):
+            for half in range(2):
+                cols = slice(half * PAIRS, (half + 1) * PAIRS)
+                nc.scalar.activation(
+                    partner[t][:, cols], dt[t][:].indirect(entries(n3_t, half * PAIRS, PAIRS)), COPY
+                )
+            width = S // pieces
+            for piece in range(pieces):
+                cols = slice(piece * width, (piece + 1) * width)
+                nc.vector.tensor_tensor(result[t][:, cols], dt[t][:, cols], partner[t][:, cols], MAX)
+                nc.sync.dma_start(out_t[t][:, cols], result[t][:, cols])
+
+        fetch_pairs(0)
+        put_sums(0)
+        put_differences(0)
+        fetch_pairs(1)
+        put_sums(1)
+        fetch_pairs(2)
+        put_sums(2)
+        put_differences(1)
+        fetch_pairs(3)
+        put_sums(3)
+        put_differences(2)
+        finish(0, 1)
+        put_differences(3)
+        finish(1, 1)
+        finish(2, 1)
+        finish(3, 2)

@@ -48,41 +48,31 @@ def tile_picked_hpqihaarh_none_p_kernel(
         xs_table = sbuf("xs_table", TABLE, U8)
         ds_table = sbuf("ds_table", TABLE, U8)
         w_scale_raw = sbuf("w_scale_raw", S, U8)
-        w_scale_spread = sbuf("w_scale_spread", S, U8)
-        w_scale = sbuf("w_scale", S, U8)
         planes = sbuf("planes", 2 * S, U8)
         gain_raw = sbuf("gain_raw", PACK, F32)
+        gain = sbuf("gain", PACK, F32)
         w_word_raw = sbuf("w_word_raw", 2 * S, U8)
         dw_table = sbuf("dw_table", TABLE, I32)
         xw_table = sbuf("xw_table", TABLE, I32)
 
-        def load_scale_rows(queue, tile, rows):
-            words = rows.shape[1] // 4
-            queue.dma_start(tile[:].bitcast(I32), rows.bitcast(I32).unsqueeze(1).to_broadcast([16, 8, words]))
-
-        def place_scale_rows(queue, plane, spread_rows):
-            for a in range(4):
-                queue.dma_start(plane[a:P:32, :].bitcast(I32), spread_rows[8 * a : P : 32, :].bitcast(I32))
-
-        nc.gpsimd.memset(planes[:].bitcast(I32), 0)
-        nc.gpsimd.memset(w_scale[:].bitcast(I32), 0)
+        nc.gpsimd.memset(ds_table[:].bitcast(I32), 0)
+        nc.vector.memset(xs_table[:].bitcast(I32), 0)
+        nc.vector.memset(w_scale_raw[:].bitcast(I32), 0)
+        nc.vector.memset(planes[:].bitcast(I32), 0)
         nc.gpsimd.dma_start(gain_raw[:], gn.rearrange("(p t) o -> p (t o)", t=PACK))
-        load_scale_rows(nc.scalar, w_scale_raw, w1_scales[0])
-        nc.scalar.dma_start(w_word_raw[:].bitcast(I32), w1_words[0].bitcast(I32))
+        for a in range(4):
+            nc.gpsimd.dma_start(w_scale_raw[a:P:32, :].bitcast(I32), w1_scales[0, a:16:4, :].bitcast(I32))
+        nc.scalar.activation(gain[:], gain_raw[:], COPY, scale=0.0625)
+        nc.sync.dma_start(ds_table[0:P:8, :].bitcast(I32), d_scales[0].bitcast(I32))
+        nc.sync.dma_start(xs_table[0:P:8, :].bitcast(I32), x_scales[0].bitcast(I32))
         k1_t = load_list("k1_t", k1)
-        load_scale_rows(nc.sync, ds_table, d_scales[0])
         offs_t = load_list("offs_t", offs)
-        load_scale_rows(nc.sync, xs_table, x_scales[0])
-        nc.sync.dma_start(dw_table[:], d_words[0].rearrange("p c r -> p (c r)").bitcast(I32))
-        nc.sync.dma_start(xw_table[:], x_words[0].rearrange("p c r -> p (c r)").bitcast(I32))
         n1_t = load_list("n1_t", n1)
         n2_t = load_list("n2_t", n2)
         n3_t = load_list("n3_t", n3)
-        nc.vector.tensor_copy(
-            w_scale_spread[:].rearrange("p (t m) -> p t m", t=PACK),
-            w_scale_raw[:].rearrange("p (m t) -> p t m", t=PACK),
-        )
-        place_scale_rows(nc.gpsimd, w_scale, w_scale_spread)
+        nc.sync.dma_start(dw_table[:], d_words[0].rearrange("p c r -> p (c r)").bitcast(I32))
+        nc.sync.dma_start(xw_table[:], x_words[0].rearrange("p c r -> p (c r)").bitcast(I32))
+        nc.sync.dma_start(w_word_raw[:].bitcast(I32), w1_words[0].bitcast(I32))
 
         ds_picked = sbuf("ds_picked", S, U8)
         xs_picked = sbuf("xs_picked", S, U8)
@@ -94,7 +84,8 @@ def tile_picked_hpqihaarh_none_p_kernel(
             ds_picked[:].rearrange("p (m t) -> p t m", t=PACK),
         )
         nc.vector.tensor_copy(spread[:, S : 2 * S].bitcast(I32), xs_picked[:].bitcast(I32))
-        place_scale_rows(nc.scalar, planes, spread)
+        for a in range(4):
+            nc.sync.dma_start(planes[a:P:32, :].bitcast(I32), spread[8 * a : P : 32, :].bitcast(I32))
 
         dw_picked = sbuf("dw_picked", S, U32)
         dw_dealt = sbuf("dw_dealt", S, U32)
@@ -110,19 +101,24 @@ def tile_picked_hpqihaarh_none_p_kernel(
                 xw_table[:].bitcast(U32).indirect(entries(offs_t, half * (S // 2), S // 2)),
             )
 
-        gain = sbuf("gain", PACK, F32)
-        nc.scalar.activation(gain[:], gain_raw[:], COPY, scale=0.0625)
         w_word = sbuf("w_word", 2 * S, U8)
         nc.scalar.copy(
             w_word[:].bitcast(U16).rearrange("p (t m) -> p t m", t=PACK),
             w_word_raw[:].bitcast(U16).rearrange("p (m t) -> p t m", t=PACK),
         )
 
+        w_scale = keep.tile([P, S], U8, name="w_scale", tag="xw_table", align_bytes=64)
+        nc.vector.tensor_copy(
+            w_scale[:].rearrange("p (t m) -> p t m", t=PACK),
+            w_scale_raw[:].rearrange("p (m t) -> p t m", t=PACK),
+        )
+
         blocks = S // BLOCK
         z = [sbuf("z%d" % b, PACK * BLOCK, BF16) for b in range(blocks)]
         z_word = sbuf("z_word", S, U32)
         z_scale = sbuf("z_scale", S, U8)
-        for b in range(blocks):
+
+        def first_product(b):
             h = psum.tile([P, PACK, BLOCK], F32, name="h%d" % b, tag="bank%d" % b)
             half, inner = divmod(b, 2)
             for t in range(PACK):
@@ -135,20 +131,34 @@ def tile_picked_hpqihaarh_none_p_kernel(
                     start=True,
                     stop=True,
                 )
+            return h
+
+        def gain_on_vector(b):
+            h = first_product(b)
+            nc.vector.tensor_tensor(
+                z[b][:].rearrange("p (j t) -> p j t", t=PACK),
+                h[:].rearrange("p t j -> p j t"),
+                gain[:].unsqueeze(1).to_broadcast([P, BLOCK, PACK]),
+                MULT,
+            )
+
+        def gain_on_scalar(b):
+            h = first_product(b)
             z_jt = z[b][:].rearrange("p (j t) -> p j t", t=PACK)
-            if b == 0:
-                for t in range(PACK):
-                    nc.scalar.activation(z_jt[:, :, t], h[:, t, :], COPY, scale=gain[:, t : t + 1])
-            else:
-                nc.vector.tensor_tensor(
-                    z_jt,
-                    h[:].rearrange("p t j -> p j t"),
-                    gain[:].unsqueeze(1).to_broadcast([P, BLOCK, PACK]),
-                    MULT,
-                )
-        for b in (1, 2, 0, 3):
+            for t in range(PACK):
+                nc.scalar.activation(z_jt[:, :, t], h[:, t, :], COPY, scale=gain[:, t : t + 1])
+
+        def quantise(b):
             cols = slice(b * BLOCK, (b + 1) * BLOCK)
             nc.vector.quantize_mx(z_word[:, cols].bitcast(FP8X4), z_scale[:, cols], z[b][:])
+
+        gain_on_vector(0)
+        gain_on_scalar(2)
+        quantise(0)
+        gain_on_vector(1)
+        gain_on_vector(3)
+        for b in range(1, blocks):
+            quantise(b)
 
         def second(acc, t, first, count):
             nc.tensor.matmul_mx(
@@ -170,11 +180,11 @@ def tile_picked_hpqihaarh_none_p_kernel(
         result = [sbuf("result%d" % t, S, F32) for t in range(PACK)]
         out_t = out.rearrange("(p t) j -> t p j", t=PACK)
 
-        early = psum.tile([P, S - BLOCK], F32, name="early", tag="bank4")
-        late = psum.tile([P, BLOCK], F32, name="late", tag="bank5")
-        for b in (1, 2, 0):
-            second(early[:, b * BLOCK : (b + 1) * BLOCK], 0, b * BLOCK, BLOCK)
-        second(late[:], 0, S - BLOCK, BLOCK)
+        early = psum.tile([P, S // 2], F32, name="early", tag="bank4")
+        late = psum.tile([P, S // 2], F32, name="late", tag="bank5")
+        for b in range(blocks):
+            half, inner = divmod(b, 2)
+            second((early, late)[half][:, inner * BLOCK : (inner + 1) * BLOCK], 0, b * BLOCK, BLOCK)
         acc2 = [None]
         for t in range(1, PACK):
             acc = psum.tile([P, S], F32, name="acc%d" % t, tag=("bank6", "bank7", "bank0")[t - 1])
@@ -183,8 +193,8 @@ def tile_picked_hpqihaarh_none_p_kernel(
 
         def fetch_pairs(t):
             if t == 0:
-                nc.scalar.copy(h2[0][:, 0 : S - BLOCK], early[:])
-                nc.scalar.copy(h2[0][:, S - BLOCK : S], late[:])
+                nc.scalar.copy(h2[0][:, 0 : S // 2], early[:])
+                nc.vector.tensor_copy(h2[0][:, S // 2 : S], late[:])
                 nc.vector.tensor_copy(pa[0][:], h2[0][:].indirect(n1_t[:]))
             else:
                 nc.scalar.copy(h2[t][:], acc2[t][:])

@@ -11,6 +11,8 @@ U8 = mybir.dt.uint8
 FP8X4 = mybir.dt.float8_e4m3fn_x4
 FP4X4 = mybir.dt.float4_e2m1fn_x4
 COPY = mybir.ActivationFunctionType.Copy
+RELU = mybir.ActivationFunctionType.Relu
+SUBTRACT = mybir.AluOpType.subtract
 ADD = mybir.AluOpType.add
 MULT = mybir.AluOpType.mult
 MAX = mybir.AluOpType.max
@@ -19,9 +21,14 @@ P = 128
 PACK = 4
 TABLE = 2048
 S = 512
-PAIRS = 256
+HALF = S // 2
 BLOCK = 128
+BLOCKS = S // BLOCK
 LIST_ROWS = 16
+SCALE_ROWS = 16
+QUADRANT = 32
+ROW_STEP = P // SCALE_ROWS
+SCALAR_BLOCK = 2
 
 FLOPS = 2 * 2 * 512 * 512 * 512
 
@@ -60,11 +67,13 @@ def tile_picked_hpqihaarh_none_p_kernel(
         nc.vector.memset(w_scale_raw[:].bitcast(I32), 0)
         nc.vector.memset(planes[:].bitcast(I32), 0)
         nc.gpsimd.dma_start(gain_raw[:], gn.rearrange("(p t) o -> p (t o)", t=PACK))
-        for a in range(4):
-            nc.gpsimd.dma_start(w_scale_raw[a:P:32, :].bitcast(I32), w1_scales[0, a:16:4, :].bitcast(I32))
+        for a in range(PACK):
+            nc.gpsimd.dma_start(
+                w_scale_raw[a:P:QUADRANT, :].bitcast(I32), w1_scales[0, a:SCALE_ROWS:PACK, :].bitcast(I32)
+            )
         nc.scalar.activation(gain[:], gain_raw[:], COPY, scale=0.0625)
-        nc.sync.dma_start(ds_table[0:P:8, :].bitcast(I32), d_scales[0].bitcast(I32))
-        nc.sync.dma_start(xs_table[0:P:8, :].bitcast(I32), x_scales[0].bitcast(I32))
+        nc.sync.dma_start(ds_table[0:P:ROW_STEP, :].bitcast(I32), d_scales[0].bitcast(I32))
+        nc.sync.dma_start(xs_table[0:P:ROW_STEP, :].bitcast(I32), x_scales[0].bitcast(I32))
         k1_t = load_list("k1_t", k1)
         offs_t = load_list("offs_t", offs)
         n1_t = load_list("n1_t", n1)
@@ -84,8 +93,10 @@ def tile_picked_hpqihaarh_none_p_kernel(
             ds_picked[:].rearrange("p (m t) -> p t m", t=PACK),
         )
         nc.vector.tensor_copy(spread[:, S : 2 * S].bitcast(I32), xs_picked[:].bitcast(I32))
-        for a in range(4):
-            nc.sync.dma_start(planes[a:P:32, :].bitcast(I32), spread[8 * a : P : 32, :].bitcast(I32))
+        for a in range(PACK):
+            nc.sync.dma_start(
+                planes[a:P:QUADRANT, :].bitcast(I32), spread[ROW_STEP * a : P : QUADRANT, :].bitcast(I32)
+            )
 
         dw_picked = sbuf("dw_picked", S, U32)
         dw_dealt = sbuf("dw_dealt", S, U32)
@@ -94,11 +105,11 @@ def tile_picked_hpqihaarh_none_p_kernel(
             dw_dealt[:].rearrange("p (t c i) -> p c t i", t=PACK, i=4),
             dw_picked[:].rearrange("p (c i t) -> p c t i", t=PACK, i=4),
         )
-        xw_picked = [sbuf("xw_picked%d" % half, S // 2, U32) for half in range(2)]
+        xw_picked = [sbuf("xw_picked%d" % half, HALF, U32) for half in range(2)]
         for half in range(2):
             nc.vector.tensor_copy(
                 xw_picked[half][:],
-                xw_table[:].bitcast(U32).indirect(entries(offs_t, half * (S // 2), S // 2)),
+                xw_table[:].bitcast(U32).indirect(entries(offs_t, half * HALF, HALF)),
             )
 
         w_word = sbuf("w_word", 2 * S, U8)
@@ -106,15 +117,13 @@ def tile_picked_hpqihaarh_none_p_kernel(
             w_word[:].bitcast(U16).rearrange("p (t m) -> p t m", t=PACK),
             w_word_raw[:].bitcast(U16).rearrange("p (m t) -> p t m", t=PACK),
         )
-
         w_scale = keep.tile([P, S], U8, name="w_scale", tag="xw_table", align_bytes=64)
         nc.vector.tensor_copy(
             w_scale[:].rearrange("p (t m) -> p t m", t=PACK),
             w_scale_raw[:].rearrange("p (m t) -> p t m", t=PACK),
         )
 
-        blocks = S // BLOCK
-        z = [sbuf("z%d" % b, PACK * BLOCK, BF16) for b in range(blocks)]
+        z = [sbuf("z%d" % b, PACK * BLOCK, BF16) for b in range(BLOCKS)]
         z_word = sbuf("z_word", S, U32)
         z_scale = sbuf("z_scale", S, U8)
 
@@ -153,14 +162,15 @@ def tile_picked_hpqihaarh_none_p_kernel(
             nc.vector.quantize_mx(z_word[:, cols].bitcast(FP8X4), z_scale[:, cols], z[b][:])
 
         gain_on_vector(0)
-        gain_on_scalar(2)
+        gain_on_scalar(SCALAR_BLOCK)
         quantise(0)
-        gain_on_vector(1)
-        gain_on_vector(3)
-        for b in range(1, blocks):
+        for b in range(1, BLOCKS):
+            if b != SCALAR_BLOCK:
+                gain_on_vector(b)
+        for b in range(1, BLOCKS):
             quantise(b)
 
-        def second(acc, t, first, count):
+        def second_product(acc, t, first, count):
             nc.tensor.matmul_mx(
                 acc,
                 lhsT=w_word[:, 2 * t * P : 2 * (t + 1) * P].bitcast(FP4X4),
@@ -172,53 +182,61 @@ def tile_picked_hpqihaarh_none_p_kernel(
             )
 
         h2 = [sbuf("h2_%d" % t, S, F32) for t in range(PACK)]
-        pa = [sbuf("pa%d" % t, PAIRS, F32) for t in range(PACK)]
-        pb = [sbuf("pb%d" % t, PAIRS, F32) for t in range(PACK)]
-        neg_pb = [sbuf("neg_pb%d" % t, PAIRS, F32) for t in range(PACK)]
+        pa = [sbuf("pa%d" % t, HALF, F32) for t in range(PACK)]
+        pb = [sbuf("pb%d" % t, HALF, F32) for t in range(PACK)]
         dt = [sbuf("dt%d" % t, S, F32) for t in range(PACK)]
-        partner = [sbuf("partner%d" % t, S, F32) for t in range(PACK)]
         result = [sbuf("result%d" % t, S, F32) for t in range(PACK)]
-        out_t = out.rearrange("(p t) j -> t p j", t=PACK)
+        out_slots = out.rearrange("(p t) j -> t p j", t=PACK)
 
-        early = psum.tile([P, S // 2], F32, name="early", tag="bank4")
-        late = psum.tile([P, S // 2], F32, name="late", tag="bank5")
-        for b in range(blocks):
+        early = psum.tile([P, HALF], F32, name="early", tag="bank4")
+        late = psum.tile([P, HALF], F32, name="late", tag="bank5")
+        for b in range(BLOCKS):
             half, inner = divmod(b, 2)
-            second((early, late)[half][:, inner * BLOCK : (inner + 1) * BLOCK], 0, b * BLOCK, BLOCK)
-        acc2 = [None]
-        for t in range(1, PACK):
-            acc = psum.tile([P, S], F32, name="acc%d" % t, tag=("bank6", "bank7", "bank0")[t - 1])
-            second(acc[:], t, 0, S)
-            acc2.append(acc)
+            second_product((early, late)[half][:, inner * BLOCK : (inner + 1) * BLOCK], 0, b * BLOCK, BLOCK)
+        whole = {}
+        for t, bank in ((1, "bank6"), (2, "bank7"), (3, "bank0")):
+            whole[t] = psum.tile([P, S], F32, name="acc%d" % t, tag=bank)
+            second_product(whole[t][:], t, 0, S)
 
         def fetch_pairs(t):
             if t == 0:
-                nc.scalar.copy(h2[0][:, 0 : S // 2], early[:])
-                nc.vector.tensor_copy(h2[0][:, S // 2 : S], late[:])
+                nc.scalar.copy(h2[0][:, 0:HALF], early[:])
+                nc.vector.tensor_copy(h2[0][:, HALF:S], late[:])
                 nc.vector.tensor_copy(pa[0][:], h2[0][:].indirect(n1_t[:]))
             else:
-                nc.scalar.copy(h2[t][:], acc2[t][:])
+                nc.scalar.copy(h2[t][:], whole[t][:])
                 nc.scalar.activation(pa[t][:], h2[t][:].indirect(n1_t[:]), COPY)
             nc.scalar.activation(pb[t][:], h2[t][:].indirect(n2_t[:]), COPY)
 
         def put_sums(t):
-            nc.vector.tensor_tensor(dt[t][:].indirect(n1_t[:]), pa[t][:], pb[t][:], ADD)
+            sums = sbuf("sums%d" % t, HALF, F32)
+            engine = nc.vector if t == 0 else nc.gpsimd
+            engine.tensor_tensor(sums[:], pa[t][:], pb[t][:], ADD)
+            nc.vector.tensor_copy(dt[t][:].indirect(n1_t[:]), sums[:])
 
         def put_differences(t):
-            nc.scalar.activation(neg_pb[t][:], pb[t][:], COPY, scale=-1.0)
-            nc.vector.tensor_tensor(dt[t][:].indirect(n2_t[:]), pa[t][:], neg_pb[t][:], ADD)
+            tag = "h2_%d" % (t + 1) if t in (1, 2) else "differences%d" % t
+            differences = keep.tile([P, HALF], F32, name="differences%d" % t, tag=tag, align_bytes=64)
+            nc.gpsimd.tensor_tensor(differences[:], pa[t][:], pb[t][:], SUBTRACT)
+            nc.vector.tensor_copy(dt[t][:].indirect(n2_t[:]), differences[:])
 
-        def finish(t, pieces):
+        def fetch_partners(t):
+            partner = sbuf("partner%d" % t, S, F32)
             for half in range(2):
-                cols = slice(half * PAIRS, (half + 1) * PAIRS)
                 nc.scalar.activation(
-                    partner[t][:, cols], dt[t][:].indirect(entries(n3_t, half * PAIRS, PAIRS)), COPY
+                    partner[:, half * HALF : (half + 1) * HALF],
+                    dt[t][:].indirect(entries(n3_t, half * HALF, HALF)),
+                    COPY,
                 )
+            return partner
+
+        def finish_on_vector(t, pieces):
+            partner = fetch_partners(t)
             width = S // pieces
             for piece in range(pieces):
                 cols = slice(piece * width, (piece + 1) * width)
-                nc.vector.tensor_tensor(result[t][:, cols], dt[t][:, cols], partner[t][:, cols], MAX)
-                nc.sync.dma_start(out_t[t][:, cols], result[t][:, cols])
+                nc.vector.tensor_tensor(result[t][:, cols], dt[t][:, cols], partner[:, cols], MAX)
+                nc.sync.dma_start(out_slots[t][:, cols], result[t][:, cols])
 
         fetch_pairs(0)
         put_sums(0)
@@ -228,11 +246,16 @@ def tile_picked_hpqihaarh_none_p_kernel(
         fetch_pairs(2)
         put_sums(2)
         put_differences(1)
+        lead = sbuf("lead", S, F32)
+        nc.gpsimd.tensor_tensor(lead[:], fetch_partners(0)[:], dt[0][:], SUBTRACT)
         fetch_pairs(3)
         put_sums(3)
         put_differences(2)
-        finish(0, 1)
         put_differences(3)
-        finish(1, 1)
-        finish(2, 1)
-        finish(3, 2)
+        excess = sbuf("excess", S, F32)
+        nc.scalar.activation(excess[:], lead[:], RELU)
+        nc.gpsimd.tensor_tensor(result[0][:], dt[0][:], excess[:], ADD)
+        nc.sync.dma_start(out_slots[0], result[0][:])
+        finish_on_vector(1, 1)
+        finish_on_vector(2, 1)
+        finish_on_vector(3, 2)

from contextlib import ExitStack

import concourse.mybir as mybir

F32 = mybir.dt.float32
BF16 = mybir.dt.bfloat16
I32 = mybir.dt.int32
U32 = mybir.dt.uint32
U16 = mybir.dt.uint16
U8 = mybir.dt.uint8
FP8X4 = mybir.dt.float8_e4m3fn_x4
FP4X4 = mybir.dt.float4_e2m1fn_x4
COPY = mybir.ActivationFunctionType.Copy
RELU = mybir.ActivationFunctionType.Relu
SUBTRACT = mybir.AluOpType.subtract
ADD = mybir.AluOpType.add
MULT = mybir.AluOpType.mult
MAX = mybir.AluOpType.max

P = 128
PACK = 4
TABLE = 2048
S = 512
HALF = S // 2
BLOCK = 128
BLOCKS = S // BLOCK
LIST_ROWS = 16
SCALE_ROWS = 16
QUADRANT = 32
ROW_STEP = P // SCALE_ROWS
SCALAR_BLOCK = 2

FLOPS = 2 * 2 * 512 * 512 * 512


def tile_picked_hpqihaarh_none_p_kernel(
    tc, x_words, x_scales, d_words, d_scales, gn, w1_words, w1_scales, offs, k1, n1, n2, n3, out
):
    nc = tc.nc
    with ExitStack() as ctx:
        keep = ctx.enter_context(tc.tile_pool(name="keep", bufs=1))
        psum = ctx.enter_context(tc.psum_pool(name="psum", bufs=1))

        def sbuf(name, columns, dtype):
            return keep.tile([P, columns], dtype, name=name, align_bytes=64)

        def load_list(name, dram):
            tile = keep.tile(list(dram.shape), U16, name=name)
            nc.sync.dma_start(tile[:], dram)
            return tile

        def entries(list_tile, first, count):
            return list_tile[:, first // LIST_ROWS : (first + count) // LIST_ROWS]

        xs_table = sbuf("xs_table", TABLE, U8)
        ds_table = sbuf("ds_table", TABLE, U8)
        w_scale_raw = sbuf("w_scale_raw", S, U8)
        planes = sbuf("planes", 2 * S, U8)
        gain_raw = sbuf("gain_raw", PACK, F32)
        gain = sbuf("gain", PACK, F32)
        w_word_raw = sbuf("w_word_raw", 2 * S, U8)
        dw_table = sbuf("dw_table", TABLE, I32)
        xw_table = sbuf("xw_table", TABLE, I32)

        nc.gpsimd.memset(ds_table[:].bitcast(I32), 0)
        nc.vector.memset(xs_table[:].bitcast(I32), 0)
        nc.vector.memset(w_scale_raw[:].bitcast(I32), 0)
        nc.vector.memset(planes[:].bitcast(I32), 0)
        nc.gpsimd.dma_start(gain_raw[:], gn.rearrange("(p t) o -> p (t o)", t=PACK))
        for a in range(PACK):
            nc.gpsimd.dma_start(
                w_scale_raw[a:P:QUADRANT, :].bitcast(I32), w1_scales[0, a:SCALE_ROWS:PACK, :].bitcast(I32)
            )
        nc.scalar.activation(gain[:], gain_raw[:], COPY, scale=0.0625)
        nc.sync.dma_start(ds_table[0:P:ROW_STEP, :].bitcast(I32), d_scales[0].bitcast(I32))
        nc.sync.dma_start(xs_table[0:P:ROW_STEP, :].bitcast(I32), x_scales[0].bitcast(I32))
        k1_t = load_list("k1_t", k1)
        offs_t = load_list("offs_t", offs)
        n1_t = load_list("n1_t", n1)
        n2_t = load_list("n2_t", n2)
        n3_t = load_list("n3_t", n3)
        nc.sync.dma_start(dw_table[:], d_words[0].rearrange("p c r -> p (c r)").bitcast(I32))
        nc.sync.dma_start(xw_table[:], x_words[0].rearrange("p c r -> p (c r)").bitcast(I32))
        nc.sync.dma_start(w_word_raw[:].bitcast(I32), w1_words[0].bitcast(I32))

        ds_picked = sbuf("ds_picked", S, U8)
        xs_picked = sbuf("xs_picked", S, U8)
        spread = sbuf("spread", 2 * S, U8)
        nc.vector.tensor_copy(ds_picked[:], ds_table[:].indirect(k1_t[:]))
        nc.vector.tensor_copy(xs_picked[:], xs_table[:].indirect(offs_t[:]))
        nc.vector.tensor_copy(
            spread[:, 0:S].rearrange("p (t m) -> p t m", t=PACK),
            ds_picked[:].rearrange("p (m t) -> p t m", t=PACK),
        )
        nc.vector.tensor_copy(spread[:, S : 2 * S].bitcast(I32), xs_picked[:].bitcast(I32))
        for a in range(PACK):
            nc.sync.dma_start(
                planes[a:P:QUADRANT, :].bitcast(I32), spread[ROW_STEP * a : P : QUADRANT, :].bitcast(I32)
            )

        dw_picked = sbuf("dw_picked", S, U32)
        dw_dealt = sbuf("dw_dealt", S, U32)
        nc.vector.tensor_copy(dw_picked[:], dw_table[:].bitcast(U32).indirect(k1_t[:]))
        nc.vector.tensor_copy(
            dw_dealt[:].rearrange("p (t c i) -> p c t i", t=PACK, i=4),
            dw_picked[:].rearrange("p (c i t) -> p c t i", t=PACK, i=4),
        )
        xw_picked = [sbuf("xw_picked%d" % half, HALF, U32) for half in range(2)]
        for half in range(2):
            nc.vector.tensor_copy(
                xw_picked[half][:],
                xw_table[:].bitcast(U32).indirect(entries(offs_t, half * HALF, HALF)),
            )

        w_word = sbuf("w_word", 2 * S, U8)
        nc.scalar.copy(
            w_word[:].bitcast(U16).rearrange("p (t m) -> p t m", t=PACK),
            w_word_raw[:].bitcast(U16).rearrange("p (m t) -> p t m", t=PACK),
        )
        w_scale = keep.tile([P, S], U8, name="w_scale", tag="xw_table", align_bytes=64)
        nc.vector.tensor_copy(
            w_scale[:].rearrange("p (t m) -> p t m", t=PACK),
            w_scale_raw[:].rearrange("p (m t) -> p t m", t=PACK),
        )

        z = [sbuf("z%d" % b, PACK * BLOCK, BF16) for b in range(BLOCKS)]
        z_word = sbuf("z_word", S, U32)
        z_scale = sbuf("z_scale", S, U8)

        def first_product(b):
            h = psum.tile([P, PACK, BLOCK], F32, name="h%d" % b, tag="bank%d" % b)
            half, inner = divmod(b, 2)
            for t in range(PACK):
                nc.tensor.matmul_mx(
                    h[:, t, :],
                    lhsT=dw_dealt[:, t * P : (t + 1) * P].bitcast(FP8X4),
                    lhsT_scale=planes[:, t * P : (t + 1) * P],
                    rhs=xw_picked[half][:, inner * BLOCK : (inner + 1) * BLOCK].bitcast(FP8X4),
                    rhs_scale=planes[:, S + b * BLOCK : S + (b + 1) * BLOCK],
                    start=True,
                    stop=True,
                )
            return h

        def gain_on_vector(b):
            h = first_product(b)
            nc.vector.tensor_tensor(
                z[b][:].rearrange("p (j t) -> p j t", t=PACK),
                h[:].rearrange("p t j -> p j t"),
                gain[:].unsqueeze(1).to_broadcast([P, BLOCK, PACK]),
                MULT,
            )

        def gain_on_scalar(b):
            h = first_product(b)
            z_jt = z[b][:].rearrange("p (j t) -> p j t", t=PACK)
            for t in range(PACK):
                nc.scalar.activation(z_jt[:, :, t], h[:, t, :], COPY, scale=gain[:, t : t + 1])

        def quantise(b):
            cols = slice(b * BLOCK, (b + 1) * BLOCK)
            nc.vector.quantize_mx(z_word[:, cols].bitcast(FP8X4), z_scale[:, cols], z[b][:])

        gain_on_vector(0)
        gain_on_scalar(SCALAR_BLOCK)
        quantise(0)
        for b in range(1, BLOCKS):
            if b != SCALAR_BLOCK:
                gain_on_vector(b)
        for b in range(1, BLOCKS):
            quantise(b)

        def second_product(acc, t, first, count):
            nc.tensor.matmul_mx(
                acc,
                lhsT=w_word[:, 2 * t * P : 2 * (t + 1) * P].bitcast(FP4X4),
                lhsT_scale=w_scale[:, t * P : (t + 1) * P],
                rhs=z_word[:, first : first + count].bitcast(FP8X4),
                rhs_scale=z_scale[:, first : first + count],
                start=True,
                stop=True,
            )

        h2 = [sbuf("h2_%d" % t, S, F32) for t in range(PACK)]
        pa = [sbuf("pa%d" % t, HALF, F32) for t in range(PACK)]
        pb = [sbuf("pb%d" % t, HALF, F32) for t in range(PACK)]
        dt = [sbuf("dt%d" % t, S, F32) for t in range(PACK)]
        result = [sbuf("result%d" % t, S, F32) for t in range(PACK)]
        out_slots = out.rearrange("(p t) j -> t p j", t=PACK)

        early = psum.tile([P, HALF], F32, name="early", tag="bank4")
        late = psum.tile([P, HALF], F32, name="late", tag="bank5")
        for b in range(BLOCKS):
            half, inner = divmod(b, 2)
            second_product((early, late)[half][:, inner * BLOCK : (inner + 1) * BLOCK], 0, b * BLOCK, BLOCK)
        whole = {}
        for t, bank in ((1, "bank6"), (2, "bank7"), (3, "bank0")):
            whole[t] = psum.tile([P, S], F32, name="acc%d" % t, tag=bank)
            second_product(whole[t][:], t, 0, S)

        def fetch_pairs(t):
            if t == 0:
                nc.scalar.copy(h2[0][:, 0:HALF], early[:])
                nc.vector.tensor_copy(h2[0][:, HALF:S], late[:])
                nc.vector.tensor_copy(pa[0][:], h2[0][:].indirect(n1_t[:]))
            else:
                nc.scalar.copy(h2[t][:], whole[t][:])
                nc.scalar.activation(pa[t][:], h2[t][:].indirect(n1_t[:]), COPY)
            nc.scalar.activation(pb[t][:], h2[t][:].indirect(n2_t[:]), COPY)

        def put_sums(t):
            sums = sbuf("sums%d" % t, HALF, F32)
            engine = nc.vector if t == 0 else nc.gpsimd
            engine.tensor_tensor(sums[:], pa[t][:], pb[t][:], ADD)
            nc.vector.tensor_copy(dt[t][:].indirect(n1_t[:]), sums[:])

        def put_differences(t):
            tag = "h2_%d" % (t + 1) if t in (1, 2) else "differences%d" % t
            differences = keep.tile([P, HALF], F32, name="differences%d" % t, tag=tag, align_bytes=64)
            nc.gpsimd.tensor_tensor(differences[:], pa[t][:], pb[t][:], SUBTRACT)
            nc.vector.tensor_copy(dt[t][:].indirect(n2_t[:]), differences[:])

        def fetch_partners(t):
            partner = sbuf("partner%d" % t, S, F32)
            for half in range(2):
                nc.scalar.activation(
                    partner[:, half * HALF : (half + 1) * HALF],
                    dt[t][:].indirect(entries(n3_t, half * HALF, HALF)),
                    COPY,
                )
            return partner

        def finish_on_vector(t, pieces):
            partner = fetch_partners(t)
            width = S // pieces
            for piece in range(pieces):
                cols = slice(piece * width, (piece + 1) * width)
                nc.vector.tensor_tensor(result[t][:, cols], dt[t][:, cols], partner[:, cols], MAX)
                nc.sync.dma_start(out_slots[t][:, cols], result[t][:, cols])

        fetch_pairs(0)
        put_sums(0)
        put_differences(0)
        fetch_pairs(1)
        put_sums(1)
        fetch_pairs(2)
        put_sums(2)
        put_differences(1)
        lead = sbuf("lead", S, F32)
        nc.gpsimd.tensor_tensor(lead[:], fetch_partners(0)[:], dt[0][:], SUBTRACT)
        fetch_pairs(3)
        put_sums(3)
        put_differences(2)
        put_differences(3)
        excess = sbuf("excess", S, F32)
        nc.scalar.activation(excess[:], lead[:], RELU)
        nc.gpsimd.tensor_tensor(result[0][:], dt[0][:], excess[:], ADD)
        nc.sync.dma_start(out_slots[0], result[0][:])
        finish_on_vector(1, 1)
        finish_on_vector(2, 1)
        finish_on_vector(3, 2)
